import numpy as np
CORES = [125,127,253,255,381,383,509,511]
N = 8
RM, R, T = 131072, 4096, 512
CAPP = 128
def entries(a): return a.T.reshape(-1)
def pack(v, P): return np.ascontiguousarray(np.asarray(v, np.int32).reshape(-1, P).T)
def owners(rng, how):
    if how == "alike": return np.stack([rng.permutation(np.repeat(rng.permutation(N)[:T // CAPP], CAPP)) for r in range(N)])
    if how == "full": p = np.repeat(rng.permutation(N)[:T // CAPP], CAPP); return np.stack([rng.permutation(p) for r in range(N)])
    return np.stack([rng.permutation(np.repeat(np.arange(N), CAPP))[:T] for r in range(N)])
def lists(rng, how):
    M = rng.integers(0, N * R, N * RM)
    O1 = owners(rng, how); O2 = rng.permutation(N)[O1] if how in ("alike", "full") else owners(rng, "uniform")
    sl = np.stack([1 + rng.permutation(RM - 2)[:N * T] for o in range(N)])
    if how == "edge": sl[:, 0] = 0; sl[:, 1] = RM - 1
    I = np.zeros((N, T), np.int64); took = np.zeros(N, np.int64)
    for r in range(N):
        for o in range(N): m = np.nonzero(O1[r] == o)[0]; I[r, m] = RM * o + sl[o, took[o]:took[o] + len(m)]; took[o] += len(m)
    A = R * O2 + (np.where(rng.random((N, T)) < 0.5, 0, R - 1) if how == "edge" else rng.integers(0, R, (N, T)))
    if how == "alike": I = RM * O1 + sl[O1, 0]; A = R * O2 + rng.integers(0, R, N)[O1]
    M[I.reshape(-1)] = A.reshape(-1)
    if how == "sorted": I = np.sort(I, axis=1)
    if how == "full":
        I[1::3] = np.sort(I[1::3], axis=1); I[2::3] = np.sort(I[2::3], axis=1).reshape(-1, 16, T // 16).transpose(0, 2, 1).reshape(-1, T)
    return {"mp": np.stack([pack(m, 16) for m in M.reshape(N, RM)]), "idx": np.stack([pack(i, 16) for i in I])}
def setup_inputs(rng):
    return dict({"tab": rng.standard_normal((N, 128, R), dtype=np.float32)}, **lists(rng, "uniform"))
def setup_inputs_alike(rng):
    d = setup_inputs(rng); d.update(lists(rng, "alike"))
    for k in ("tab",): d[k] = (d[k].astype(np.float32) * 1048576.0).astype(d[k].dtype)
    return d
def setup_inputs_edge(rng):
    d = setup_inputs(rng); d.update(lists(rng, "edge"))
    for k in ("tab",): d[k] = (d[k].astype(np.float32) * (1 / 1024.0)).astype(d[k].dtype)
    return d
def setup_inputs_full(rng):
    d = setup_inputs(rng); d.update(lists(rng, "full"))
    return d
def setup_inputs_sorted(rng):
    d = setup_inputs(rng); d.update(lists(rng, "sorted"))
    return d
def check_inputs(x):
    bad = []
    if x["mp"].min() < 0 or x["mp"].max() >= N * R: bad.append("mp out of range")
    if x["idx"].min() < 0 or x["idx"].max() >= N * RM: bad.append("idx out of range")
    M = np.concatenate([entries(m) for m in x["mp"]])
    if max(int(np.bincount(entries(a) // RM, minlength=N).max()) for a in x["idx"]) > CAPP: bad.append("more than CAPP entries of a list point into one rank's part of the map")
    if max(int(np.bincount(M[entries(a)] // R, minlength=N).max()) for a in x["idx"]) > CAPP: bad.append("more than CAPP entries of a list have map values in one rank's part of the table")
    return bad
def reference(tab, mp, idx):
    A = np.concatenate(list(tab), axis=1)
    M = np.concatenate([entries(m) for m in mp])
    return {"y": np.stack([A[:, M[entries(idx[r])]] for r in range(N)])}

from concourse.bass import DstId, RemoteDMATransfer
from concourse.mybir import AluOpType, ActivationFunctionType

A = AluOpType
COPY = ActivationFunctionType.Copy
N = 8
DTYPES = {"F": "float32", "I": "int32", "B": "bfloat16", "U": "uint16"}
BANKS = ["b%d" % k for k in range(8)]

SCRATCH, PLACE = {}, {}
for _s in ("X I 4", "mapi I 1024", "mapf F 1024", "tabs F 4096", "OFF U 1024", "VA I 64", "VT I 16", "HV0 I 2", "land F 1024", "HD F 256",
           "MK F 1024", "GM F 1024", "Y F 512", "DA F 256", "DB F 512", "DC F 128"):
    _n, _d, _c = _s.split()
    SCRATCH[_n] = ("sbuf", [128, int(_c)], DTYPES[_d])
    PLACE[_n] = (_n, 0, int(_c), DTYPES[_d])
_pool = ("pI I 1;pbI I 4;pF F 1;pbF F 4;i128 B 128;i16 B 128;O32 B 32;M8 B 32;T64 B 64;T64p B 64;I16 I 512;I8 I 256;neg B 128;tri B 128;"
         "one B 128;oneF F 132;idw F 132;r4i B 32;r8i B 64;r4 B 32;r8 B 64;k32 I 32;k16 I 16;z4 F 4;rep16 U 32;rep8 U 16;rm4 U 2;rm8 U 4;"
         "pA U 2;pV U 2;tmA F 1;tmV F 1;REP F 128;WR F 128;KK F 32;own I 4;FI I 8;FF F 8;sB I 4;qB I 4;P1 F 4;PF F 4;m32 B 32;in32 B 32;"
         "pr F 32;s16 F 16;s8 F 8;ADR I 4;BI I 8;BF F 8;oaP F 4;SLI I 4;SL F 4;L1 B 512;R1 B 1536;DG B 512;OHS F 512;MM F 32;M64 B 64;"
         "in64 B 64;p64 F 64;z32 F 32;z16 F 16;zz F 8;e32 F 32;e16 F 16;e8 F 8;ze F 4;zk F 32;offW U 32").split(";")
for _w, _n in (("A", 16), ("B", 32), ("C", 16)):
    _pool += ["%s%s %s %d" % (_k, _w, _d, _n * _f) for _k, _d, _f in (
        ("Vc", "I", 1), ("hi", "I", 1), ("lo", "I", 1), ("m", "B", 1), ("inc", "B", 1), ("sl", "I", 1), ("b", "I", 1), ("a", "I", 1),
        ("lm", "F", 1), ("OB", "F", 16), ("OA", "F", 8), ("RH", "F", 8), ("c16", "F", 1), ("of", "U", 1))]
_size = {_d: 0 for _d in DTYPES}
for _s in _pool:
    _n, _d, _c = _s.split()
    PLACE[_n] = ("pool" + _d, _size[_d], int(_c), DTYPES[_d])
    _size[_d] += -(-int(_c) // 8) * 8
for _d in DTYPES:
    SCRATCH["pool" + _d] = ("sbuf", [128, _size[_d]], DTYPES[_d])
for _n in BANKS:
    SCRATCH[_n] = ("psum", [128, 512], "float32")
    PLACE[_n] = (_n, 0, 512, "float32")

SEMAPHORES = ["cg", "cv", "cs", "ct", "ldx", "ldm", "ld0", "ld1", "ld2", "ld3", "sty", "sts", "lsL", "ls0", "ls1", "lsR"]
SEMAPHORES += ["%s%d" % (_s, _k) for _s in ("L", "M0", "M1", "M2", "D") for _k in range(N)]


def tracker(g, T):
    eng = {"g": g, "v": g.vector, "s": g.scalar, "t": g.tensor, "y": g.sync}
    cnt = {"g": 0, "v": 0, "s": 0, "t": 0}
    know = {q: {} for q in eng}
    acc = {}

    def wait(q, tok):
        sem, val, clk = tok
        if know[q].get(sem, 0) < val:
            eng[q].wait_ge(T.sem[sem], val)
            for s, v in list(clk.items()) + [(sem, val)]:
                know[q][s] = max(v, know[q].get(s, 0))

    def deps(q, reads, writes, accum=False):
        for buf, c0, c1 in reads:
            for e in acc.get(buf, []):
                if e[0] < c1 and c0 < e[1] and (e[2] or (buf in BANKS and e[3] != q)):
                    wait(q, e[4])
        for buf, c0, c1 in writes:
            for e in acc.get(buf, []):
                if e[0] < c1 and c0 < e[1] and not (accum and e[3] == q):
                    wait(q, e[4])

    def record(q, tok, reads, writes):
        for buf, c0, c1 in writes:
            acc[buf] = [e for e in acc.get(buf, []) if not (c0 <= e[0] and e[1] <= c1)] + [(c0, c1, True, q, tok)]
        for buf, c0, c1 in reads:
            acc.setdefault(buf, []).append((c0, c1, False, q, tok))

    def op(q, fn, reads, writes, accum=False):
        reads, writes = [[(x[0], 0, 512) if x[0] in BANKS else x[:3] for x in z] for z in (reads, writes)]
        deps(q, reads, writes, accum)
        cnt[q] += 1
        fn(eng[q]).then_inc(T.sem["c" + q], 1)
        record(q, ("c" + q, cnt[q], dict(know[q])), reads, writes)

    def dma(q, out, in_, sem, reads, writes):
        deps(q, reads, writes)
        eng[q].dma_start(out, in_).then_inc(T.sem[sem], 16)
        record(q, (sem, 16, dict(know[q])), reads, writes)

    def finish(extra):
        for sem, val in [("c" + q, cnt[q]) for q in cnt] + extra:
            g.wait_ge(T.sem[sem], val)
    return op, dma, lambda sem, val, writes: record("x", (sem, val, {}), [], writes), lambda reads: deps("g", reads, []), finish, wait


def bits(m):
    return [k for k in range(16) if m >> k & 1]


def split(mask, n):
    e = bits(mask)
    k = len(e) // n
    return [sum(1 << x for x in e[i * k:(i + 1) * k]) for i in range(n)]


def relations(core, T, topo):
    rel = {"own": [], "R": [], "C": [], "D": []}
    for k, c in enumerate(T.cores):
        a, b = topo.host(c), topo.host(core)
        rel["own" if a == b else "R" if topo.rack(a) == topo.rack(b) else "C" if topo.may_write(core, c) else "D"].append(k)
    return rel


def relay_of(s, T, topo):
    src = T.cores[s]
    rel = relations(src, T, topo)
    second = rel["own"].index(s)
    via = T.cores[rel["C" if second else "R"][0]]
    cand = [c for c in range(via - 16, via + 16) if c >= 0 and c < 512 and T.rank_of(c) is None
            and topo.host(c) == topo.host(via) and topo.chip(c) == topo.chip(via) and topo.die(c) != topo.die(via)
            and topo.may_write(src, c) and all(topo.may_write(c, T.cores[d]) for d in rel["D"])]
    return cand[-1] if second else cand[0]


def dest(c, core, topo):
    rid, pid = topo.addr(c, core)
    return DstId(rid=rid, pnc=pid)


def relay_program(g, core, s, T, topo):
    src = T.cores[s]
    D = [T.cores[d] for d in relations(src, T, topo)["D"]]
    mask = topo.mask(core, D[0])
    got, n, sent = len(bits(topo.mask(src, core))), len(bits(mask)), 0
    for m, name, c0, c1, oname, o0 in (("L", "OFF", s * 128, s * 128 + 128, "OFF", s * 128), ("M0", "HV0", 0, 2, "VT", s * 2),
                                       ("M2", "VA", s * 8, s * 8 + 8, "VA", s * 8), ("D", "HD", 0, 256, "land", s * 128)):
        sm = T.sem["%s%d" % (m, s)]
        g.wait_ge(sm, got)
        if m == "D":
            tr = [RemoteDMATransfer(dst_ids=[dest(d, core, topo)], dma_engine_mask=split(mask, 2)[k], remote_sem=sm,
                                    srcs=[T.HD[:, k * 128:k * 128 + 128]], dsts=[T.land[:, o0:o0 + 128]]) for k, d in enumerate(D)]
        else:
            tr = [RemoteDMATransfer(dst_ids=[dest(d, core, topo) for d in D], dma_engine_mask=mask, remote_sem=sm,
                                    srcs=[T[name][:, c0:c1]], dsts=[T[oname][:, o0:o0 + c1 - c0] for d in D])]
        g.remote_dma_fused(tr, local_sem=T.sem.lsR)
        sent += n
    g.wait_ge(T.sem.lsR, sent)


def rank_program(g, core, T, topo):
    r = T.rank_of(core)
    if r is None:
        for s in range(N):
            if core not in T.cores and abs(core - T.cores[0]) % 128 < 16 or abs(core - T.cores[0]) % 128 > 112:
                if relay_of(s, T, topo) == core:
                    relay_program(g, core, s, T, topo)
        return
    rel = relations(core, T, topo)
    own, near = rel["own"], rel["R"] + rel["C"]
    ci = own.index(r)
    mate = own[1 - ci]
    H = relay_of(r, T, topo)
    op, dma, ext, need, finish, wait = tracker(g, T)
    mask = topo.mask(core, T.cores[near[0]])
    ne = len(bits(mask))

    def ap(x):
        buf, o = PLACE[x[0]][:2]
        return T[buf][0:x[3], o + x[1]:o + x[2]] if len(x) > 3 else T[buf][:, o + x[1]:o + x[2]]

    def F(n, a=0, b=None):
        return (n, a, PLACE[n][2] if b is None else b)

    def ind(x, i):
        return ap(x).indirect(ap(i)) if i else ap(x)

    def ts(out, in0, s1, s2, o0, *o1):
        sc = [ap(x) if isinstance(x, tuple) else x for x in (s1, s2)]
        op("v", lambda e: e.tensor_scalar(ap(out), ap(in0), sc[0], sc[1], o0, *o1), [in0] + [x for x in (s1, s2) if isinstance(x, tuple)], [out])

    def tt(out, a, b, o, i=None):
        op("v", lambda e: e.tensor_tensor(ap(out), ind(a, i), ap(b), o), [a, b] + ([i] if i else []), [out])

    def cp(out, in_, i=None):
        op("v", lambda e: e.tensor_copy(ap(out), ind(in_, i)), [in_] + ([i] if i else []), [out])

    def act(out, in_, i):
        op("s", lambda e: e.activation(ap(out), ind(in_, i), COPY), [in_, i], [out])

    def ms(n, v):
        op("v", lambda e: e.memset(ap(F(n)), v), [], [F(n)])

    def iota(n, pat, base=0, cm=0):
        kw = {} if PLACE[n][3] == "int32" else {"allow_small_or_imprecise_dtypes": True}
        op("g", lambda e: e.iota(ap(F(n)), pat, base, cm, **kw), [], [F(n)])

    def select(n, src, width, cmp, base):
        op("g", lambda e: e.affine_select(ap(F(n)), ap(F(src)), [[-1, width]], cmp, 0.0, base, 1), [F(src)], [F(n)])

    def mm(out, l, rh, start, stop):
        op("t", lambda e: e.matmul(ap(out), ap(l), ap(rh), start, stop), [l, rh], [out], accum=True)

    def scan(out, d0, d1):
        op("v", lambda e: e.tensor_tensor_scan(ap(out), ap(d0), ap(d1), 0.0, A.mult, A.add), [d0, d1], [out])

    def send(parts, sem, lsem):
        need([p[0] for p in parts])
        g.remote_dma_fused([RemoteDMATransfer(dst_ids=[dest(c, core, topo) for c, _ in ds], dma_engine_mask=m,
                                              remote_sem=T.sem["%s%d" % (sem, r)], srcs=[ap(x)], dsts=[d for _, d in ds])
                            for x, ds, m in parts], local_sem=T.sem[lsem])

    def cores(ks):
        return [T.cores[k] for k in ks]

    dma("y", T.X[:], T.idx[:], "ldx", [], [F("X")])
    dma("y", T.mapi[:], T.mp[:], "ldm", [], [F("mapi")])

    def tab(k):
        x = ("tabs", k * 1024, k * 1024 + 1024)
        dma("y", ap(x), T.tab[:, x[1]:x[2]], "ld%d" % k, [], [x])
    tab(0)

    for k in range(N):
        if k != r:
            ext("L%d" % k, ne, [("OFF", k * 128, k * 128 + 128)])
            ext("M2%d" % k, ne, [("VA", k * 8, k * 8 + 8)])
            ext("D%d" % k, ne if k == mate else ne // 4 if k in near else ne // 2, [("land", k * 128, k * 128 + 128)])
            if k != mate:
                ext("%s%d" % ("M1" if k in near else "M0", k), ne // 2 if k in near else ne, [("VT", k * 2, k * 2 + 2)])

    iota("pI", [[1, 1]], 0, 1)
    iota("O32", [[1, 8], [0, 4]])
    iota("r4i", [[0, 8], [1, 4]])
    ms("neg", -1.0)
    ms("one", 1.0)
    select("tri", "neg", 128, A.is_ge, 0)
    iota("i16", [[0, 8], [1, 16]])
    iota("i128", [[1, 128]])
    ms("oneF", 1.0)
    select("idw", "oneF", 132, A.is_equal, 1)
    ts(("pbI", 0, 1), F("pI"), 3, None, A.bitwise_and)
    ts(("pbI", 1, 2), F("pI"), 7, None, A.bitwise_and)
    ts(("pbI", 2, 3), F("pI"), 3, 1, A.logical_shift_right, A.bitwise_and)
    ts(("pbI", 3, 4), F("pI"), 3, None, A.logical_shift_right)
    ts(F("r4"), F("r4i"), 1.0, None, A.min)
    ms("z4", 0.0)
    cp(F("pbF"), F("pbI"))
    ts(F("rm4"), ("z4", 0, 2), ("pbF", 0, 1), None, A.add)
    cp(F("pF"), F("pI"))

    X = F("X")
    ts(F("own"), X, 17, None, A.logical_shift_right)
    ts(("FI", 0, 4), X, 4, 992, A.logical_shift_right, A.bitwise_and)
    ts(("FI", 4, 8), X, 4, 31, A.logical_shift_right, A.bitwise_and)
    tt(F("m32"), F("own"), F("O32"), A.is_equal, F("rm4"))
    ts(F("sB"), X, 14, 7, A.logical_shift_right, A.bitwise_and)
    ts(F("qB"), X, 15, None, A.bitwise_and)
    scan(F("in32"), F("r4"), F("m32"))
    mm(("b0", 0, 32), F("one"), F("O32"), True, False)
    mm(("b0", 0, 32), F("tri"), F("m32"), False, False)
    mm(("b0", 0, 32), F("one"), F("in32"), False, True)
    cp(F("FF"), F("FI"))
    ts(F("P1"), F("qB"), 8.0, 1.0, A.mult, A.add)
    tt(F("PF"), F("P1"), F("sB"), A.add)
    tt(F("pr"), ("b0", 0, 32), F("m32"), A.mult)
    tt(F("s16"), ("pr", 0, 16), ("pr", 16, 32), A.add)
    tt(F("s8"), ("s16", 0, 8), ("s16", 8, 16), A.add)
    tt(F("ADR"), ("s8", 0, 4), ("s8", 4, 8), A.add)
    ts(("BI", 0, 4), F("ADR"), 15, None, A.bitwise_and)
    ts(("BI", 4, 8), F("ADR"), 4, None, A.logical_shift_right)
    cp(F("BF"), F("BI"))
    ts(F("oaP"), ("BI", 4, 8), 64.0, None, A.add)
    for c in range(4):
        l = ("L1", c * 128, c * 128 + 128)
        ts(l, F("i16"), ("BF", c, c + 1), None, A.is_equal)
        for k, (oa, val) in enumerate(((("BF", 4 + c, 5 + c), ("FF", c, c + 1)), (("BF", 4 + c, 5 + c), ("FF", 4 + c, 5 + c)),
                                       (("oaP", c, c + 1), ("PF", c, c + 1)))):
            o = (c * 3 + k) * 128
            ts(("R1", o, o + 128), F("i128"), oa, val, A.is_equal, A.mult)
            mm(("b1", 0, 128), l, ("R1", o, o + 128), c == 0 and k == 0, c == 3 and k == 2)
    x = ("OFF", r * 128, r * 128 + 128)
    cp(x, ("b1", 0, 128))
    send([(x, [(c, ap(x)) for c in cores([mate] + near) + [H]], mask)], "L", "lsL")
    wait("y", ("lsL", ne, {}))
    tab(1)
    tab(2)

    def look(k, bank, col):
        o = k * 128
        act(("MK", o, o + 128), F("idw"), ("OFF", o + 64 + r * 8, o + 72 + r * 8))
        tt(("GM", o, o + 128), F("mapf"), ("MK", o, o + 128), A.mult, ("OFF", o + r * 8, o + r * 8 + 8))
        mm((bank, col, col + 1), ("GM", o, o + 128), ("oneF", 0, 1), True, True)

    def V(p):
        return ("VA", r * 8 + rel[p][0], r * 8 + rel[p][0] + 2)

    ts(F("mapf"), F("mapi"), 4096.0, None, A.add)
    look(r, "b3", ci)
    iota("M8", [[0, 4], [1, 8]])
    iota("k16", [[2, 16]])
    iota("k32", [[1, 32]])
    ts(F("rep8"), F("k16"), ("pbF", 2, 3), None, A.add)
    ts(F("SLI"), F("ADR"), 127, None, A.bitwise_and)
    cp(F("SL"), F("SLI"))
    for c in range(4):
        ts(("DG", c * 128, c * 128 + 128), ("idw", 1, 129), ("SL", c, c + 1), None, A.mult)
    mm(("b2", 0, 512), F("one"), F("DG"), True, True)
    look(mate, "b3", 1 - ci)
    cp(V("own"), ("b3", 0, 2))
    send([(V("own"), [(H, T.HV0[:])], mask)], "M0", "ls0")
    iota("I16", [[0, 32], [1, 16]])
    iota("I8", [[0, 32], [1, 8]])
    iota("r8i", [[0, 8], [1, 8]])
    iota("T64", [[1, 8], [0, 8]])
    iota("T64p", [[1, 8], [0, 8]], 1)
    ts(F("OHS"), ("b2", 0, 512), F("pF"), None, A.is_equal)
    tt(F("MM"), F("own"), F("M8"), A.is_equal, ("rep8", 0, 2))
    for k, p in enumerate("RC"):
        for j in range(2):
            look(rel[p][j], "b4", 2 * k + j)
    for k, p in enumerate("RC"):
        cp(V(p), ("b4", 2 * k, 2 * k + 2))
    vt = T.VT[:, r * 2:r * 2 + 2]
    send([(V(p), [(c, vt) for c in cores(rel[to])], m) for p, to, m in zip("RC", "CR", split(mask, 2))], "M1", "ls1")
    wait("y", ("ls1", ne, {}))
    tab(3)
    cp(F("rep16"), F("k32"))
    ts(F("r8"), F("r8i"), 1.0, None, A.min)
    ts(F("rm8"), F("z4"), ("pbF", 1, 2), None, A.add)
    ts(F("tmA"), ("pbF", 1, 2), 2.0, ("pbF", 2, 3), A.mult, A.add)
    ts(F("tmV"), ("pbF", 1, 2), 8.0, ("pbF", 2, 3), A.mult, A.add)
    cp(("pA", 0, 1), F("tmA"))
    cp(("pV", 0, 1), F("tmV"))
    ts(F("REP"), F("i16"), F("pF"), None, A.is_equal)
    ts(F("WR"), F("i16"), ("pbF", 3, 4), None, A.is_equal)
    ts(F("KK"), F("O32"), ("pbF", 1, 2), None, A.is_equal)
    for j in range(2):
        look(rel["D"][j], "b5", j)
    cp(V("D"), ("b5", 0, 2))
    cp(("VT", r * 2, r * 2 + 2), ("b5", 0, 2))
    x = ("VA", r * 8, r * 8 + 8)
    send([(x, [(c, ap(x)) for c in cores([mate] + near) + [H]], mask)], "M2", "ls0")

    def wave(W, n, banks, load):
        load()
        yield
        ts(F("hi" + W), F("Vc" + W), 12, None, A.logical_shift_right)
        yield
        ts(F("m" + W), F("hi" + W), float(r + 1), None, A.is_equal)
        yield
        scan(F("inc" + W), ("r8", 0, n), F("m" + W))
        mm((banks[0], 0, n), F("tri"), F("m" + W), True, False)
        mm((banks[0], 0, n), F("one"), F("inc" + W), False, True)
        yield
        ts(F("lo" + W), F("Vc" + W), 4095, None, A.bitwise_and)
        yield
        tt(F("lm" + W), F("lo" + W), F("m" + W), A.mult)
        yield
        cp(F("sl" + W), (banks[0], 0, n))
        yield
        ts(F("a" + W), F("sl" + W), 4, None, A.logical_shift_right)
        ts(F("b" + W), F("sl" + W), 15, None, A.bitwise_and)
        yield
        tt(F("OA" + W), F("a" + W), ("I8", 0, n * 8), A.is_equal, ("rep8", 0, n // 2))
        yield
        tt(F("OB" + W), F("b" + W), ("I16", 0, n * 16), A.is_equal, ("rep16", 0, n))
        yield
        tt(F("RH" + W), F("lm" + W), F("OA" + W), A.mult, ("rep8", 0, n // 2))
        for c in range(n):
            mm((banks[1], c // 8 * 8, c // 8 * 8 + 8, 16), ("OB" + W, c * 16, c * 16 + 16), ("RH" + W, c * 8, c * 8 + 8), c % 8 == 0, c % 8 == 7)
        yield
        cp(("c16" + W, 0, n, 16), (banks[1], 0, n, 16))
        mm((banks[2], 0, n), ("REP", 0, 128, 16), ("c16" + W, 0, n, 16), True, True)
        yield
        cp(F("of" + W), (banks[2], 0, n))
        yield

    def run(*gens):
        live = list(gens)
        while live:
            for x in list(live):
                if next(x, "end") == "end":
                    live.remove(x)

    def pair(dst, c0, p):
        cp((dst, c0, c0 + 16), ("VA", rel[p][0], rel[p][0] + 58), ("pV", 0, 1))

    def loadA():
        cp(("VT", mate * 2, mate * 2 + 2), ("VA", mate * 8 + rel["D"][0], mate * 8 + rel["D"][0] + 2))
        cp(F("VcA"), F("VT"), ("pA", 0, 1))

    def loadB():
        pair("VcB", 0, "R")
        pair("VcB", 16, "C")
    tb = F("tabs")
    block = T.land[:, r * 128:r * 128 + 128]
    run(wave("A", 16, ("b0", "b1", "b6"), loadA))
    cp(("DA", 0, 128), tb, ("ofA", 0, 8))
    act(("DA", 128, 256), tb, ("ofA", 8, 16))
    send([(F("DA"), [(H, T.HD[:])], mask)], "D", "ls0")
    run(wave("B", 32, ("b7", "b3", "b4"), loadB))
    for q in range(2):
        cp(("DB", q * 128, q * 128 + 128), tb, ("ofB", q * 8, q * 8 + 8))
        act(("DB", 256 + q * 128, 384 + q * 128), tb, ("ofB", 16 + q * 8, 24 + q * 8))
    send([(("DB", q * 128, q * 128 + 128), [(T.cores[k], block)], split(mask, 4)[q]) for q, k in enumerate(near)], "D", "ls0")

    def zgen():
        tt(F("M64"), ("hiC", ci * 8, ci * 8 + 8), F("T64p"), A.is_equal, F("rm8"))
        yield
        scan(F("in64"), F("r8"), F("M64"))
        mm(("b2", 0, 64), F("one"), F("T64"), True, False)
        mm(("b2", 0, 64), F("tri"), F("M64"), False, False)
        mm(("b2", 0, 64), F("one"), F("in64"), False, True)
        yield
        tt(F("p64"), ("b2", 0, 64), F("M64"), A.mult)
        yield
        tt(F("z32"), ("p64", 0, 32), ("p64", 32, 64), A.add)
        yield
        tt(F("z16"), ("z32", 0, 16), ("z32", 16, 32), A.add)
        yield
        tt(F("zz"), ("z16", 0, 8), ("z16", 8, 16), A.add)
        for c in range(4):
            mm(("b7", c * 8, c * 8 + 8), ("OHS", c * 128, c * 128 + 128), F("zz"), True, True)
        yield
        tt(F("e32"), ("b7", 0, 32), F("MM"), A.mult)
        yield
        for a, b, n in (("e32", "e16", 16), ("e16", "e8", 8), ("e8", "ze", 4)):
            buf, o = PLACE[a][:2]
            op("v", lambda e: e.tensor_tensor(ap(F(b)), T[buf][:, o:o + 2 * n:2], T[buf][:, o + 1:o + 2 * n:2], A.add), [F(a)], [F(b)])
            yield
        tt(F("zk"), F("ze"), F("KK"), A.mult, F("rm4"))
        mm(("b3", 0, 32), F("WR"), F("zk"), True, True)
        yield
        cp(F("offW"), ("b3", 0, 32))
        yield

    wc = wave("C", 16, ("b0", "b1", "b6"), lambda: pair("VcC", 0, "own"))
    next(wc)
    next(wc)
    run(wc, zgen())
    cp(("land", r * 128, r * 128 + 128), tb, ("ofC", ci * 8, ci * 8 + 8))
    act(F("DC"), tb, ("ofC", 8 - ci * 8, 16 - ci * 8))
    send([(F("DC"), [(T.cores[mate], block)], mask)], "D", "ls0")

    cp(("Y", 0, 256), F("land"), ("offW", 0, 16))
    act(("Y", 256, 512), F("land"), ("offW", 16, 32))
    dma("y", T.y[:, 0:256], T.Y[:, 0:256], "sty", [("Y", 0, 256)], [])
    dma("s", T.y[:, 256:512], T.Y[:, 256:512], "sts", [("Y", 256, 512)], [])
    finish([("lsL", ne), ("ls0", 5 * ne), ("ls1", ne), ("sty", 16), ("sts", 16)])
